import numpy as np, ml_dtypes
CORES = [56,61,80,85]
N = 4
T, M = 2048, 256
def entries(a): return a.T.reshape(-1)
def pack(v, P): return np.ascontiguousarray(np.asarray(v, np.int32).reshape(-1, P).T)
def lists(rng, how):
    I = rng.integers(0, N * T, (N, 8, M))
    if how == "alike": I[:] = rng.integers(0, N * T, (N, 8, 1))
    if how == "same": I[:] = rng.integers(0, N * T, (N, 1, M))
    if how == "hotrank": I = T * int(rng.integers(N)) + rng.integers(0, T, (N, 8, M))
    if how == "own": I = T * np.arange(N).reshape(N, 1, 1) + rng.integers(0, T, (N, 8, M))
    if how == "edge": I = T * rng.integers(0, N, (N, 8, M)) + np.where(rng.random((N, 8, M)) < 0.5, 0, T - 1)
    return {"idx": np.stack([np.concatenate([pack(I[r, h], 16) for h in range(8)], axis=0) for r in range(N)])}
def setup_inputs(rng):
    return dict({"x": rng.standard_normal((N, 128, T), dtype=np.float32).astype(ml_dtypes.bfloat16)}, **lists(rng, "uniform"))
def setup_inputs_alike(rng):
    d = setup_inputs(rng); d.update(lists(rng, "alike"))
    for k in ("x",): d[k] = (d[k].astype(np.float32) * 1048576.0).astype(d[k].dtype)
    return d
def setup_inputs_edge(rng):
    d = setup_inputs(rng); d.update(lists(rng, "edge"))
    for k in ("x",): d[k] = (d[k].astype(np.float32) * (1 / 1024.0)).astype(d[k].dtype)
    return d
def setup_inputs_hotrank(rng):
    d = setup_inputs(rng); d.update(lists(rng, "hotrank"))
    return d
def setup_inputs_own(rng):
    d = setup_inputs(rng); d.update(lists(rng, "own"))
    return d
def setup_inputs_same(rng):
    d = setup_inputs(rng); d.update(lists(rng, "same"))
    return d
def check_inputs(x):
    bad = []
    if x["idx"].min() < 0 or x["idx"].max() >= N * T: bad.append("idx out of range")
    return bad
def reference(x, idx):
    A = np.concatenate(list(x), axis=1)
    y = np.zeros((N, 128, M), x.dtype)
    for r in range(N):
        for h in range(8): y[r][16 * h:16 * h + 16] = A[16 * h:16 * h + 16][:, entries(idx[r][16 * h:16 * h + 16])]
    return {"y": y}

@@ -1,0 +1,158 @@
+from concourse.bass import DstId, RemoteDMATransfer
+from concourse.mybir import AluOpType
+
+COLS = 2048
+M = 256
+K = 16
+HALF = COLS // 2
+
+SCRATCH = {
+    "ix": ("sbuf", [128, K], "int32"),
+    "rq": ("sbuf", [128, K], "int32"),
+    "tab": ("sbuf", [128, COLS], "bfloat16"),
+    "off": ("sbuf", [128, K], "uint16"),
+    "res": ("sbuf", [128, M], "bfloat16"),
+    "own": ("sbuf", [128, K], "uint16"),
+    "land": ("sbuf", [128, 4 * M], "bfloat16"),
+    "ia": ("sbuf", [128, K], "int32"),
+    "ib": ("sbuf", [128, K], "int32"),
+    "o2": ("sbuf", [128, K], "int32"),
+    "off2": ("sbuf", [128, K], "uint16"),
+    "yb": ("sbuf", [128, M], "bfloat16"),
+}
+SEMAPHORES = ["s_idx", "s_x0", "s_x1", "s_io", "s_j1", "s_j2", "s_own", "s_o2", "s_o3", "s_o4", "s_og",
+              "s_fw", "s_rq", "s_tab", "s_cv", "s_res", "s_land", "s_y", "s_st", "s_loc"]
+
+
+def _plan(T, topo):
+    ranks = list(T.cores)
+    chips = sorted(set(topo.chip(c) for c in ranks))
+    assert len(chips) == 2
+    on = {ch: [c for c in ranks if topo.chip(c) == ch] for ch in chips}
+    near, far, helpers = {}, {}, {}
+    for s in ranks:
+        near[s] = on[topo.chip(s)]
+        far[s] = on[[ch for ch in chips if ch != topo.chip(s)][0]]
+        cand = [h for h in range(topo.CORES_PER_CHIP * topo.CHIPS)
+                if topo.chip(h) == topo.chip(s) and topo.die(h) == topo.die(s) and h not in ranks
+                and all(topo.may_write(h, t) for t in far[s])]
+        assert len(cand) >= len(far[s])
+        helpers[s] = cand[:len(far[s])]
+    return near, far, helpers
+
+
+def _mask(topo, src, dst, lo, n):
+    m = topo.mask(src, dst)
+    es = [e for e in range(m.bit_length()) if (m >> e) & 1]
+    assert lo + n <= len(es)
+    return sum(1 << e for e in es[lo:lo + n])
+
+
+def _width(topo, src, dst):
+    m = topo.mask(src, dst)
+    return sum((m >> e) & 1 for e in range(m.bit_length()))
+
+
+def _xfer(topo, src, dst, lo, n, sem, out_ap, in_ap):
+    rid, pid, _se = topo.addr(dst)
+    return RemoteDMATransfer(dst_ids=[DstId(rid=rid, pnc=pid)], dma_engine_mask=_mask(topo, src, dst, lo, n),
+                             remote_sem=sem, src=in_ap, dst=out_ap)
+
+
+def _send(g, topo, src, dst, n, sem, loc, out_ap, in_ap):
+    rid, pid, _se = topo.addr(dst)
+    g.remote_dma(out_ap, in_ap, sem, loc, pid, rid, _mask(topo, src, dst, 0, n))
+
+
+def _answer(g, T, owner, n_rq, tab_waits):
+    S, V = T.sem, g.vector
+    V.wait_ge(S.s_rq, n_rq)
+    V.tensor_scalar(T.off[:], T.rq[:], COLS * owner, COLS - 1, AluOpType.subtract, AluOpType.min).then_inc(S.s_cv, 1)
+    V.wait_ge(S.s_cv, 1)
+    for sem, n in tab_waits:
+        V.wait_ge(sem, n)
+    V.tensor_copy(T.res[:], T.tab[:, 0:COLS].indirect(T.off[:, 0:K])).then_inc(S.s_res, 1)
+
+
+def _helper(g, core, T, topo, s, t, partner):
+    S = T.sem
+    w = _width(topo, core, partner)
+    slot = M * T.rank_of(s)
+    g.wait_ge(S.s_fw, 4)
+    _send(g, topo, core, partner, w, S.s_rq, S.s_loc, T.rq[:], T.ix[:])
+    _answer(g, T, T.rank_of(s), w, [(S.s_tab, 16)])
+    g.wait_ge(S.s_res, 1)
+    _send(g, topo, core, t, w, S.s_land, S.s_loc, T.land[:, slot:slot + M], T.res[:])
+    g.wait_ge(S.s_loc, 2 * w)
+
+
+def _rank(g, core, T, topo, near, far, helpers):
+    S, V = T.sem, g.vector
+    r = T.rank_of(core)
+    hs = helpers[core]
+    peer = [c for c in near[core] if c != core][0]
+    slot = M * r
+
+    g.sync.dma_start(T.ix[:], T.idx[:]).then_inc(S.s_idx, 16)
+    g.scalar.dma_start(T.tab[:, 0:HALF], T.x[:, 0:HALF]).then_inc(S.s_x0, 16)
+    g.sync.dma_start(T.tab[:, HALF:COLS], T.x[:, HALF:COLS]).then_inc(S.s_x1, 16)
+
+    g.iota(T.ia[:], [[16, K]], 0, 1).then_inc(S.s_io, 1)
+    g.iota(T.ib[:], [[0, K]], 0, 1).then_inc(S.s_io, 1)
+
+    loc = 0
+    g.wait_ge(S.s_idx, 16)
+    g.remote_dma_fused([_xfer(topo, core, h, 4 * i, 4, S.s_fw, T.ix[:], T.ix[:]) for i, h in enumerate(hs)],
+                       local_sem=S.s_loc)
+    loc += 4 * len(hs)
+    for sem, a in ((S.s_x0, 0), (S.s_x1, HALF)):
+        g.wait_ge(sem, 16)
+        g.remote_dma_fused([_xfer(topo, core, h, 8 * i, 8, S.s_tab, T.tab[:, a:a + HALF], T.tab[:, a:a + HALF])
+                            for i, h in enumerate(hs)], local_sem=S.s_loc)
+        loc += 8 * len(hs)
+    _send(g, topo, core, peer, 8, S.s_rq, S.s_loc, T.rq[:], T.ix[:])
+    loc += 8
+
+    V.wait_ge(S.s_io, 2)
+    V.tensor_scalar(T.ib[:], T.ib[:], 0x70, None, AluOpType.bitwise_and).then_inc(S.s_j1, 1)
+    V.wait_ge(S.s_j1, 1)
+    V.tensor_tensor(T.ia[:], T.ia[:], T.ib[:], AluOpType.subtract).then_inc(S.s_j2, 1)
+    V.wait_ge(S.s_idx, 16)
+    V.tensor_scalar(T.own[:], T.ix[:], COLS * r, COLS - 1, AluOpType.subtract, AluOpType.min).then_inc(S.s_own, 1)
+    V.tensor_scalar(T.o2[:], T.ix[:], 3, 0x700, AluOpType.arith_shift_right, AluOpType.bitwise_and).then_inc(S.s_o2, 1)
+    V.wait_ge(S.s_o2, 1)
+    V.wait_ge(S.s_j2, 1)
+    V.tensor_tensor(T.o2[:], T.o2[:], T.ia[:], AluOpType.add).then_inc(S.s_o3, 1)
+    V.wait_ge(S.s_o3, 1)
+    V.tensor_copy(T.off2[:], T.o2[:]).then_inc(S.s_o4, 1)
+    V.wait_ge(S.s_own, 1)
+    V.wait_ge(S.s_x0, 16)
+    V.wait_ge(S.s_x1, 16)
+    V.tensor_copy(T.land[:, slot:slot + M], T.tab[:, 0:COLS].indirect(T.own[:, 0:K])).then_inc(S.s_og, 1)
+    _answer(g, T, r, 8, [])
+    g.wait_ge(S.s_res, 1)
+    wp = _width(topo, core, peer)
+    _send(g, topo, core, peer, wp, S.s_land, S.s_loc, T.land[:, slot:slot + M], T.res[:])
+    loc += wp
+
+    arrivals = _width(topo, peer, core) + sum(_width(topo, helpers[t][near[core].index(core)], core) for t in far[core])
+    V.wait_ge(S.s_land, arrivals)
+    V.wait_ge(S.s_og, 1)
+    V.wait_ge(S.s_o4, 1)
+    V.tensor_copy(T.yb[:], T.land[:, 0:4 * M].indirect(T.off2[:, 0:K])).then_inc(S.s_y, 1)
+    g.sync.wait_ge(S.s_y, 1)
+    g.sync.dma_start(T.y[:], T.yb[:]).then_inc(S.s_st, 16)
+    g.sync.wait_ge(S.s_st, 16)
+    g.wait_ge(S.s_loc, loc)
+
+
+def rank_program(g, core, T, topo):
+    near, far, helpers = _plan(T, topo)
+    if T.rank_of(core) is not None:
+        _rank(g, core, T, topo, near, far, helpers)
+        return
+    for s in T.cores:
+        for k, h in enumerate(helpers[s]):
+            if h == core:
+                t = far[s][k]
+                _helper(g, core, T, topo, s, t, helpers[t][near[s].index(s)])

@@ -1,12 +1,15 @@
 from concourse.bass import DstId, RemoteDMATransfer
-from concourse.mybir import AluOpType
+from concourse.mybir import AluOpType, ActivationFunctionType
 
 COLS = 2048
 M = 256
 K = 16
-HALF = COLS // 2
+CH = 2
+E1 = 2
+PIECE = COLS // CH
 
 SCRATCH = {
+    "ixd": ("dram", [128, K], "int32"),
     "ix": ("sbuf", [128, K], "int32"),
     "rq": ("sbuf", [128, K], "int32"),
     "tab": ("sbuf", [128, COLS], "bfloat16"),
@@ -20,8 +23,8 @@ SCRATCH = {
     "off2": ("sbuf", [128, K], "uint16"),
     "yb": ("sbuf", [128, M], "bfloat16"),
 }
-SEMAPHORES = ["s_idx", "s_x0", "s_x1", "s_io", "s_j1", "s_j2", "s_own", "s_o2", "s_o3", "s_o4", "s_og",
-              "s_fw", "s_rq", "s_tab", "s_cv", "s_res", "s_land", "s_y", "s_st", "s_loc"]
+SEMAPHORES = ["s_idx", "s_ix", "s_io", "s_j1", "s_j2", "s_own", "s_o2", "s_o3", "s_o4", "s_og",
+              "s_fw", "s_rq", "s_tab", "s_cv", "s_res", "s_land", "s_y", "s_st", "s_loc"] + ["s_x%d" % i for i in range(CH)]
 
 
 def _plan(T, topo):
@@ -64,24 +67,30 @@ def _send(g, topo, src, dst, n, sem, loc, out_ap, in_ap):
     g.remote_dma(out_ap, in_ap, sem, loc, pid, rid, _mask(topo, src, dst, 0, n))
 
 
+def _gather2(g, out, win, offs, waits, sem):
+    for q in (g.vector, g.scalar):
+        for s, n in waits:
+            q.wait_ge(s, n)
+    g.vector.tensor_copy(out[:, 0:M // 2], win.indirect(offs[:, 0:K // 2])).then_inc(sem, 1)
+    g.scalar.activation(out[:, M // 2:M], win.indirect(offs[:, K // 2:K]), ActivationFunctionType.Copy,
+                        bias=-0.0, scale=1.0).then_inc(sem, 1)
+
+
 def _answer(g, T, owner, n_rq, tab_waits):
     S, V = T.sem, g.vector
     V.wait_ge(S.s_rq, n_rq)
     V.tensor_scalar(T.off[:], T.rq[:], COLS * owner, COLS - 1, AluOpType.subtract, AluOpType.min).then_inc(S.s_cv, 1)
-    V.wait_ge(S.s_cv, 1)
-    for sem, n in tab_waits:
-        V.wait_ge(sem, n)
-    V.tensor_copy(T.res[:], T.tab[:, 0:COLS].indirect(T.off[:, 0:K])).then_inc(S.s_res, 1)
+    _gather2(g, T.res, T.tab[:, 0:COLS], T.off, tab_waits + [(S.s_cv, 1)], S.s_res)
 
 
 def _helper(g, core, T, topo, s, t, partner):
     S = T.sem
     w = _width(topo, core, partner)
     slot = M * T.rank_of(s)
-    g.wait_ge(S.s_fw, 4)
-    _send(g, topo, core, partner, w, S.s_rq, S.s_loc, T.rq[:], T.ix[:])
-    _answer(g, T, T.rank_of(s), w, [(S.s_tab, 16)])
-    g.wait_ge(S.s_res, 1)
+    g.wait_ge(S.s_fw, E1)
+    _send(g, topo, core, partner, w, S.s_rq, S.s_loc, T.rq[:], T.ixd[:])
+    _answer(g, T, T.rank_of(s), w, [(S.s_tab, 8 * CH)])
+    g.wait_ge(S.s_res, 2)
     _send(g, topo, core, t, w, S.s_land, S.s_loc, T.land[:, slot:slot + M], T.res[:])
     g.wait_ge(S.s_loc, 2 * w)
 
@@ -92,32 +101,36 @@ def _rank(g, core, T, topo, near, far, helpers):
     hs = helpers[core]
     peer = [c for c in near[core] if c != core][0]
     slot = M * r
+    sx = [S["s_x%d" % i] for i in range(CH)]
 
-    g.sync.dma_start(T.ix[:], T.idx[:]).then_inc(S.s_idx, 16)
-    g.scalar.dma_start(T.tab[:, 0:HALF], T.x[:, 0:HALF]).then_inc(S.s_x0, 16)
-    g.sync.dma_start(T.tab[:, HALF:COLS], T.x[:, HALF:COLS]).then_inc(S.s_x1, 16)
+    g.sync.dma_start(T.ixd[:], T.idx[:]).then_inc(S.s_idx, 16)
+    for i in range(CH):
+        q = g.sync if i % 2 else g.scalar
+        q.dma_start(T.tab[:, i * PIECE:(i + 1) * PIECE], T.x[:, i * PIECE:(i + 1) * PIECE]).then_inc(sx[i], 16)
+    g.scalar.dma_start(T.ix[:], T.idx[:]).then_inc(S.s_ix, 16)
 
     g.iota(T.ia[:], [[16, K]], 0, 1).then_inc(S.s_io, 1)
     g.iota(T.ib[:], [[0, K]], 0, 1).then_inc(S.s_io, 1)
 
     loc = 0
     g.wait_ge(S.s_idx, 16)
-    g.remote_dma_fused([_xfer(topo, core, h, 4 * i, 4, S.s_fw, T.ix[:], T.ix[:]) for i, h in enumerate(hs)],
+    g.remote_dma_fused([_xfer(topo, core, h, E1 * i, E1, S.s_fw, T.ixd[:], T.ixd[:]) for i, h in enumerate(hs)],
                        local_sem=S.s_loc)
-    loc += 4 * len(hs)
-    for sem, a in ((S.s_x0, 0), (S.s_x1, HALF)):
-        g.wait_ge(sem, 16)
-        g.remote_dma_fused([_xfer(topo, core, h, 8 * i, 8, S.s_tab, T.tab[:, a:a + HALF], T.tab[:, a:a + HALF])
+    loc += E1 * len(hs)
+    for j in range(CH):
+        a = j * PIECE
+        g.wait_ge(sx[j], 16)
+        g.remote_dma_fused([_xfer(topo, core, h, 8 * i, 8, S.s_tab, T.tab[:, a:a + PIECE], T.tab[:, a:a + PIECE])
                             for i, h in enumerate(hs)], local_sem=S.s_loc)
         loc += 8 * len(hs)
-    _send(g, topo, core, peer, 8, S.s_rq, S.s_loc, T.rq[:], T.ix[:])
+    _send(g, topo, core, peer, 8, S.s_rq, S.s_loc, T.rq[:], T.ixd[:])
     loc += 8
 
     V.wait_ge(S.s_io, 2)
     V.tensor_scalar(T.ib[:], T.ib[:], 0x70, None, AluOpType.bitwise_and).then_inc(S.s_j1, 1)
     V.wait_ge(S.s_j1, 1)
     V.tensor_tensor(T.ia[:], T.ia[:], T.ib[:], AluOpType.subtract).then_inc(S.s_j2, 1)
-    V.wait_ge(S.s_idx, 16)
+    V.wait_ge(S.s_ix, 16)
     V.tensor_scalar(T.own[:], T.ix[:], COLS * r, COLS - 1, AluOpType.subtract, AluOpType.min).then_inc(S.s_own, 1)
     V.tensor_scalar(T.o2[:], T.ix[:], 3, 0x700, AluOpType.arith_shift_right, AluOpType.bitwise_and).then_inc(S.s_o2, 1)
     V.wait_ge(S.s_o2, 1)
@@ -126,21 +139,18 @@ def _rank(g, core, T, topo, near, far, helpers):
     V.wait_ge(S.s_o3, 1)
     V.tensor_copy(T.off2[:], T.o2[:]).then_inc(S.s_o4, 1)
     V.wait_ge(S.s_own, 1)
-    V.wait_ge(S.s_x0, 16)
-    V.wait_ge(S.s_x1, 16)
+    for sem in sx:
+        V.wait_ge(sem, 16)
     V.tensor_copy(T.land[:, slot:slot + M], T.tab[:, 0:COLS].indirect(T.own[:, 0:K])).then_inc(S.s_og, 1)
-    _answer(g, T, r, 8, [])
-    g.wait_ge(S.s_res, 1)
+    _answer(g, T, r, 8, [(sem, 16) for sem in sx])
+    g.wait_ge(S.s_res, 2)
     wp = _width(topo, core, peer)
     _send(g, topo, core, peer, wp, S.s_land, S.s_loc, T.land[:, slot:slot + M], T.res[:])
     loc += wp
 
     arrivals = _width(topo, peer, core) + sum(_width(topo, helpers[t][near[core].index(core)], core) for t in far[core])
-    V.wait_ge(S.s_land, arrivals)
-    V.wait_ge(S.s_og, 1)
-    V.wait_ge(S.s_o4, 1)
-    V.tensor_copy(T.yb[:], T.land[:, 0:4 * M].indirect(T.off2[:, 0:K])).then_inc(S.s_y, 1)
-    g.sync.wait_ge(S.s_y, 1)
+    _gather2(g, T.yb, T.land[:, 0:4 * M], T.off2, [(S.s_og, 1), (S.s_o4, 1), (S.s_land, arrivals)], S.s_y)
+    g.sync.wait_ge(S.s_y, 2)
     g.sync.dma_start(T.y[:], T.yb[:]).then_inc(S.s_st, 16)
     g.sync.wait_ge(S.s_st, 16)
     g.wait_ge(S.s_loc, loc)

@@ -5,7 +5,8 @@ COLS = 2048
 M = 256
 K = 16
 CH = 2
-E1 = 2
+E1 = 4
+EX = 8
 PIECE = COLS // CH
 
 SCRATCH = {
@@ -13,17 +14,18 @@ SCRATCH = {
     "ix": ("sbuf", [128, K], "int32"),
     "rq": ("sbuf", [128, K], "int32"),
     "tab": ("sbuf", [128, COLS], "bfloat16"),
+    "both": ("sbuf", [128, 2 * COLS], "bfloat16"),
     "off": ("sbuf", [128, K], "uint16"),
     "res": ("sbuf", [128, M], "bfloat16"),
     "own": ("sbuf", [128, K], "uint16"),
-    "land": ("sbuf", [128, 4 * M], "bfloat16"),
+    "land": ("sbuf", [128, 3 * M], "bfloat16"),
     "ia": ("sbuf", [128, K], "int32"),
     "ib": ("sbuf", [128, K], "int32"),
     "o2": ("sbuf", [128, K], "int32"),
     "off2": ("sbuf", [128, K], "uint16"),
     "yb": ("sbuf", [128, M], "bfloat16"),
 }
-SEMAPHORES = ["s_idx", "s_ix", "s_io", "s_j1", "s_j2", "s_own", "s_o2", "s_o3", "s_o4", "s_og",
+SEMAPHORES = ["s_idx", "s_ix", "s_io", "s_j1", "s_j2", "s_own", "s_o1", "s_o2", "s_o3", "s_o4", "s_og",
               "s_fw", "s_rq", "s_tab", "s_cv", "s_res", "s_land", "s_y", "s_st", "s_loc"] + ["s_x%d" % i for i in range(CH)]
 
 
@@ -32,16 +34,16 @@ def _plan(T, topo):
     chips = sorted(set(topo.chip(c) for c in ranks))
     assert len(chips) == 2
     on = {ch: [c for c in ranks if topo.chip(c) == ch] for ch in chips}
-    near, far, helpers = {}, {}, {}
+    near, far, helper = {}, {}, {}
     for s in ranks:
         near[s] = on[topo.chip(s)]
         far[s] = on[[ch for ch in chips if ch != topo.chip(s)][0]]
+        assert len(near[s]) == 2 and T.rank_of(near[s][1]) == T.rank_of(near[s][0]) + 1
         cand = [h for h in range(topo.CORES_PER_CHIP * topo.CHIPS)
                 if topo.chip(h) == topo.chip(s) and topo.die(h) == topo.die(s) and h not in ranks
-                and all(topo.may_write(h, t) for t in far[s])]
-        assert len(cand) >= len(far[s])
-        helpers[s] = cand[:len(far[s])]
-    return near, far, helpers
+                and h not in helper.values() and all(topo.may_write(h, t) for t in far[s])]
+        helper[s] = cand[0]
+    return near, far, helper
 
 
 def _mask(topo, src, dst, lo, n):
@@ -76,31 +78,38 @@ def _gather2(g, out, win, offs, waits, sem):
                         bias=-0.0, scale=1.0).then_inc(sem, 1)
 
 
-def _answer(g, T, owner, n_rq, tab_waits):
+def _answer(g, T, win, first, span, n_rq, tab_waits):
     S, V = T.sem, g.vector
     V.wait_ge(S.s_rq, n_rq)
-    V.tensor_scalar(T.off[:], T.rq[:], COLS * owner, COLS - 1, AluOpType.subtract, AluOpType.min).then_inc(S.s_cv, 1)
-    _gather2(g, T.res, T.tab[:, 0:COLS], T.off, tab_waits + [(S.s_cv, 1)], S.s_res)
+    V.tensor_scalar(T.off[:], T.rq[:], first, span - 1, AluOpType.subtract, AluOpType.min).then_inc(S.s_cv, 1)
+    _gather2(g, T.res, win, T.off, tab_waits + [(S.s_cv, 1)], S.s_res)
 
 
-def _helper(g, core, T, topo, s, t, partner):
+def _slot(T, near, asker, owner):
+    n0, o = T.rank_of(near[asker][0]), T.rank_of(owner)
+    if owner in near[asker]:
+        return o - n0 + (1 if n0 > 0 else 0)
+    return 0 if n0 > 0 else 2
+
+
+def _helper(g, core, T, topo, near, s, t, partner):
     S = T.sem
     w = _width(topo, core, partner)
-    slot = M * T.rank_of(s)
+    a = M * _slot(T, near, t, s)
     g.wait_ge(S.s_fw, E1)
     _send(g, topo, core, partner, w, S.s_rq, S.s_loc, T.rq[:], T.ixd[:])
-    _answer(g, T, T.rank_of(s), w, [(S.s_tab, 8 * CH)])
+    _answer(g, T, T.both[:, 0:2 * COLS], COLS * T.rank_of(near[s][0]), 2 * COLS, w, [(S.s_tab, 2 * EX * CH)])
     g.wait_ge(S.s_res, 2)
-    _send(g, topo, core, t, w, S.s_land, S.s_loc, T.land[:, slot:slot + M], T.res[:])
+    _send(g, topo, core, t, w, S.s_land, S.s_loc, T.land[:, a:a + M], T.res[:])
     g.wait_ge(S.s_loc, 2 * w)
 
 
-def _rank(g, core, T, topo, near, far, helpers):
+def _rank(g, core, T, topo, near, far, helper):
     S, V = T.sem, g.vector
     r = T.rank_of(core)
-    hs = helpers[core]
+    place = near[core].index(core)
+    hs = [helper[core]] + [helper[c] for c in near[core] if c != core]
     peer = [c for c in near[core] if c != core][0]
-    slot = M * r
     sx = [S["s_x%d" % i] for i in range(CH)]
 
     g.sync.dma_start(T.ixd[:], T.idx[:]).then_inc(S.s_idx, 16)
@@ -112,17 +121,16 @@ def _rank(g, core, T, topo, near, far, helpers):
     g.iota(T.ia[:], [[16, K]], 0, 1).then_inc(S.s_io, 1)
     g.iota(T.ib[:], [[0, K]], 0, 1).then_inc(S.s_io, 1)
 
-    loc = 0
     g.wait_ge(S.s_idx, 16)
-    g.remote_dma_fused([_xfer(topo, core, h, E1 * i, E1, S.s_fw, T.ixd[:], T.ixd[:]) for i, h in enumerate(hs)],
-                       local_sem=S.s_loc)
-    loc += E1 * len(hs)
+    _send(g, topo, core, hs[0], E1, S.s_fw, S.s_loc, T.ixd[:], T.ixd[:])
+    loc = E1
     for j in range(CH):
         a = j * PIECE
+        b = place * COLS + a
         g.wait_ge(sx[j], 16)
-        g.remote_dma_fused([_xfer(topo, core, h, 8 * i, 8, S.s_tab, T.tab[:, a:a + PIECE], T.tab[:, a:a + PIECE])
+        g.remote_dma_fused([_xfer(topo, core, h, EX * i, EX, S.s_tab, T.both[:, b:b + PIECE], T.tab[:, a:a + PIECE])
                             for i, h in enumerate(hs)], local_sem=S.s_loc)
-        loc += 8 * len(hs)
+        loc += EX * len(hs)
     _send(g, topo, core, peer, 8, S.s_rq, S.s_loc, T.rq[:], T.ixd[:])
     loc += 8
 
@@ -132,24 +140,31 @@ def _rank(g, core, T, topo, near, far, helpers):
     V.tensor_tensor(T.ia[:], T.ia[:], T.ib[:], AluOpType.subtract).then_inc(S.s_j2, 1)
     V.wait_ge(S.s_ix, 16)
     V.tensor_scalar(T.own[:], T.ix[:], COLS * r, COLS - 1, AluOpType.subtract, AluOpType.min).then_inc(S.s_own, 1)
-    V.tensor_scalar(T.o2[:], T.ix[:], 3, 0x700, AluOpType.arith_shift_right, AluOpType.bitwise_and).then_inc(S.s_o2, 1)
+    V.tensor_scalar(T.o2[:], T.ix[:], 3, 0x700, AluOpType.arith_shift_right, AluOpType.bitwise_and).then_inc(S.s_o1, 1)
+    V.wait_ge(S.s_o1, 1)
+    if T.rank_of(near[core][0]) > 0:
+        V.tensor_scalar(T.o2[:], T.o2[:], M, M, AluOpType.max, AluOpType.subtract).then_inc(S.s_o2, 1)
+    else:
+        V.tensor_scalar(T.o2[:], T.o2[:], 2 * M, None, AluOpType.min).then_inc(S.s_o2, 1)
     V.wait_ge(S.s_o2, 1)
     V.wait_ge(S.s_j2, 1)
     V.tensor_tensor(T.o2[:], T.o2[:], T.ia[:], AluOpType.add).then_inc(S.s_o3, 1)
     V.wait_ge(S.s_o3, 1)
     V.tensor_copy(T.off2[:], T.o2[:]).then_inc(S.s_o4, 1)
+    a = M * _slot(T, near, core, core)
     V.wait_ge(S.s_own, 1)
     for sem in sx:
         V.wait_ge(sem, 16)
-    V.tensor_copy(T.land[:, slot:slot + M], T.tab[:, 0:COLS].indirect(T.own[:, 0:K])).then_inc(S.s_og, 1)
-    _answer(g, T, r, 8, [(sem, 16) for sem in sx])
+    V.tensor_copy(T.land[:, a:a + M], T.tab[:, 0:COLS].indirect(T.own[:, 0:K])).then_inc(S.s_og, 1)
+    _answer(g, T, T.tab[:, 0:COLS], COLS * r, COLS, 8, [(sem, 16) for sem in sx])
     g.wait_ge(S.s_res, 2)
     wp = _width(topo, core, peer)
-    _send(g, topo, core, peer, wp, S.s_land, S.s_loc, T.land[:, slot:slot + M], T.res[:])
+    a = M * _slot(T, near, peer, core)
+    _send(g, topo, core, peer, wp, S.s_land, S.s_loc, T.land[:, a:a + M], T.res[:])
     loc += wp
 
-    arrivals = _width(topo, peer, core) + sum(_width(topo, helpers[t][near[core].index(core)], core) for t in far[core])
-    _gather2(g, T.yb, T.land[:, 0:4 * M], T.off2, [(S.s_og, 1), (S.s_o4, 1), (S.s_land, arrivals)], S.s_y)
+    arrivals = _width(topo, peer, core) + _width(topo, helper[far[core][place]], core)
+    _gather2(g, T.yb, T.land[:, 0:3 * M], T.off2, [(S.s_og, 1), (S.s_o4, 1), (S.s_land, arrivals)], S.s_y)
     g.sync.wait_ge(S.s_y, 2)
     g.sync.dma_start(T.y[:], T.yb[:]).then_inc(S.s_st, 16)
     g.sync.wait_ge(S.s_st, 16)
@@ -157,12 +172,11 @@ def _rank(g, core, T, topo, near, far, helpers):
 
 
 def rank_program(g, core, T, topo):
-    near, far, helpers = _plan(T, topo)
+    near, far, helper = _plan(T, topo)
     if T.rank_of(core) is not None:
-        _rank(g, core, T, topo, near, far, helpers)
+        _rank(g, core, T, topo, near, far, helper)
         return
     for s in T.cores:
-        for k, h in enumerate(helpers[s]):
-            if h == core:
-                t = far[s][k]
-                _helper(g, core, T, topo, s, t, helpers[t][near[s].index(s)])
+        if helper[s] == core:
+            t = far[s][near[s].index(s)]
+            _helper(g, core, T, topo, near, s, t, helper[t])

@@ -6,6 +6,7 @@ M = 256
 K = 16
 CH = 2
 E1 = 4
+EN = 8
 EX = 8
 PIECE = COLS // CH
 
@@ -20,13 +21,15 @@ SCRATCH = {
     "own": ("sbuf", [128, K], "uint16"),
     "land": ("sbuf", [128, 3 * M], "bfloat16"),
     "ia": ("sbuf", [128, K], "int32"),
+    "pb": ("sbuf", [128, K], "int32"),
     "ib": ("sbuf", [128, K], "int32"),
     "o2": ("sbuf", [128, K], "int32"),
     "off2": ("sbuf", [128, K], "uint16"),
     "yb": ("sbuf", [128, M], "bfloat16"),
 }
-SEMAPHORES = ["s_idx", "s_ix", "s_io", "s_j1", "s_j2", "s_own", "s_o1", "s_o2", "s_o3", "s_o4", "s_og",
-              "s_fw", "s_rq", "s_tab", "s_cv", "s_res", "s_land", "s_y", "s_st", "s_loc"] + ["s_x%d" % i for i in range(CH)]
+SEMAPHORES = ["s_idx", "s_ix", "s_io", "s_ej", "s_j1", "s_j2", "s_own", "s_o1", "s_o2", "s_o3", "s_o4", "s_og",
+              "s_fw", "s_rq", "s_t0", "s_tab", "s_cv", "s_res", "s_land", "s_y", "s_st", "s_loc"] \
+             + ["s_x%d" % i for i in range(CH)]
 
 
 def _plan(T, topo):
@@ -67,6 +70,7 @@ def _xfer(topo, src, dst, lo, n, sem, out_ap, in_ap):
 def _send(g, topo, src, dst, n, sem, loc, out_ap, in_ap):
     rid, pid, _se = topo.addr(dst)
     g.remote_dma(out_ap, in_ap, sem, loc, pid, rid, _mask(topo, src, dst, 0, n))
+    return n
 
 
 def _gather2(g, out, win, offs, waits, sem):
@@ -92,16 +96,26 @@ def _slot(T, near, asker, owner):
     return 0 if n0 > 0 else 2
 
 
-def _helper(g, core, T, topo, near, s, t, partner):
+def _helper(g, core, T, topo, near, s, t, partner, other):
     S = T.sem
     w = _width(topo, core, partner)
+    peer = [c for c in near[s] if c != s][0]
     a = M * _slot(T, near, t, s)
+    b = near[s].index(s) * COLS
+    g.iota(T.ia[:], [[16, K]], 0, 1).then_inc(S.s_io, 1)
+    g.wait_ge(S.s_io, 1)
+    loc = _send(g, topo, core, s, _width(topo, core, s), S.s_ej, S.s_loc, T.ia[:], T.ia[:])
     g.wait_ge(S.s_fw, E1)
-    _send(g, topo, core, partner, w, S.s_rq, S.s_loc, T.rq[:], T.ixd[:])
-    _answer(g, T, T.both[:, 0:2 * COLS], COLS * T.rank_of(near[s][0]), 2 * COLS, w, [(S.s_tab, 2 * EX * CH)])
+    loc += _send(g, topo, core, partner, w, S.s_rq, S.s_loc, T.rq[:], T.ixd[:])
+    loc += _send(g, topo, core, peer, EN, S.s_rq, S.s_loc, T.rq[:], T.ixd[:])
+    wo = _width(topo, core, other)
+    g.wait_ge(S.s_t0, _width(topo, s, core))
+    loc += _send(g, topo, core, other, wo, S.s_tab, S.s_loc, T.both[:, b:b + PIECE], T.both[:, b:b + PIECE])
+    _answer(g, T, T.both[:, 0:2 * COLS], COLS * T.rank_of(near[s][0]), 2 * COLS, w,
+            [(S.s_t0, _width(topo, s, core)), (S.s_tab, _width(topo, other, core) + 2 * EX)])
     g.wait_ge(S.s_res, 2)
-    _send(g, topo, core, t, w, S.s_land, S.s_loc, T.land[:, a:a + M], T.res[:])
-    g.wait_ge(S.s_loc, 2 * w)
+    loc += _send(g, topo, core, t, w, S.s_land, S.s_loc, T.land[:, a:a + M], T.res[:])
+    g.wait_ge(S.s_loc, loc)
 
 
 def _rank(g, core, T, topo, near, far, helper):
@@ -111,6 +125,7 @@ def _rank(g, core, T, topo, near, far, helper):
     hs = [helper[core]] + [helper[c] for c in near[core] if c != core]
     peer = [c for c in near[core] if c != core][0]
     sx = [S["s_x%d" % i] for i in range(CH)]
+    wp = _width(topo, core, peer)
 
     g.sync.dma_start(T.ixd[:], T.idx[:]).then_inc(S.s_idx, 16)
     for i in range(CH):
@@ -118,23 +133,22 @@ def _rank(g, core, T, topo, near, far, helper):
         q.dma_start(T.tab[:, i * PIECE:(i + 1) * PIECE], T.x[:, i * PIECE:(i + 1) * PIECE]).then_inc(sx[i], 16)
     g.scalar.dma_start(T.ix[:], T.idx[:]).then_inc(S.s_ix, 16)
 
-    g.iota(T.ia[:], [[16, K]], 0, 1).then_inc(S.s_io, 1)
-    g.iota(T.ib[:], [[0, K]], 0, 1).then_inc(S.s_io, 1)
+    g.iota(T.pb[:], [[0, K]], 0, 1).then_inc(S.s_io, 1)
+    g.wait_ge(S.s_io, 1)
+    loc = _send(g, topo, core, peer, wp, S.s_ej, S.s_loc, T.ib[:], T.pb[:])
 
     g.wait_ge(S.s_idx, 16)
-    _send(g, topo, core, hs[0], E1, S.s_fw, S.s_loc, T.ixd[:], T.ixd[:])
-    loc = E1
-    for j in range(CH):
-        a = j * PIECE
-        b = place * COLS + a
-        g.wait_ge(sx[j], 16)
-        g.remote_dma_fused([_xfer(topo, core, h, EX * i, EX, S.s_tab, T.both[:, b:b + PIECE], T.tab[:, a:a + PIECE])
-                            for i, h in enumerate(hs)], local_sem=S.s_loc)
-        loc += EX * len(hs)
-    _send(g, topo, core, peer, 8, S.s_rq, S.s_loc, T.rq[:], T.ixd[:])
-    loc += 8
+    loc += _send(g, topo, core, hs[0], E1, S.s_fw, S.s_loc, T.ixd[:], T.ixd[:])
+    b = place * COLS
+    g.wait_ge(sx[0], 16)
+    loc += _send(g, topo, core, hs[0], _width(topo, core, hs[0]), S.s_t0, S.s_loc,
+                 T.both[:, b:b + PIECE], T.tab[:, 0:PIECE])
+    g.wait_ge(sx[1], 16)
+    g.remote_dma_fused([_xfer(topo, core, h, EX * i, EX, S.s_tab, T.both[:, b + PIECE:b + COLS], T.tab[:, PIECE:COLS])
+                        for i, h in enumerate(hs)], local_sem=S.s_loc)
+    loc += EX * len(hs)
 
-    V.wait_ge(S.s_io, 2)
+    V.wait_ge(S.s_ej, _width(topo, hs[0], core) + _width(topo, peer, core))
     V.tensor_scalar(T.ib[:], T.ib[:], 0x70, None, AluOpType.bitwise_and).then_inc(S.s_j1, 1)
     V.wait_ge(S.s_j1, 1)
     V.tensor_tensor(T.ia[:], T.ia[:], T.ib[:], AluOpType.subtract).then_inc(S.s_j2, 1)
@@ -156,12 +170,10 @@ def _rank(g, core, T, topo, near, far, helper):
     for sem in sx:
         V.wait_ge(sem, 16)
     V.tensor_copy(T.land[:, a:a + M], T.tab[:, 0:COLS].indirect(T.own[:, 0:K])).then_inc(S.s_og, 1)
-    _answer(g, T, T.tab[:, 0:COLS], COLS * r, COLS, 8, [(sem, 16) for sem in sx])
+    _answer(g, T, T.tab[:, 0:COLS], COLS * r, COLS, EN, [(sem, 16) for sem in sx])
     g.wait_ge(S.s_res, 2)
-    wp = _width(topo, core, peer)
     a = M * _slot(T, near, peer, core)
-    _send(g, topo, core, peer, wp, S.s_land, S.s_loc, T.land[:, a:a + M], T.res[:])
-    loc += wp
+    loc += _send(g, topo, core, peer, wp, S.s_land, S.s_loc, T.land[:, a:a + M], T.res[:])
 
     arrivals = _width(topo, peer, core) + _width(topo, helper[far[core][place]], core)
     _gather2(g, T.yb, T.land[:, 0:3 * M], T.off2, [(S.s_og, 1), (S.s_o4, 1), (S.s_land, arrivals)], S.s_y)
@@ -179,4 +191,5 @@ def rank_program(g, core, T, topo):
     for s in T.cores:
         if helper[s] == core:
             t = far[s][near[s].index(s)]
-            _helper(g, core, T, topo, near, s, t, helper[t])
+            peer = [c for c in near[s] if c != s][0]
+            _helper(g, core, T, topo, near, s, t, helper[t], helper[peer])

from concourse.bass import DstId, RemoteDMATransfer
from concourse.mybir import AluOpType, ActivationFunctionType

COLS = 2048
M = 256
K = 16
CH = 2
E1 = 4
EN = 8
EX = 8
PIECE = COLS // CH

SCRATCH = {
    "ixd": ("dram", [128, K], "int32"),
    "ix": ("sbuf", [128, K], "int32"),
    "rq": ("sbuf", [128, K], "int32"),
    "tab": ("sbuf", [128, COLS], "bfloat16"),
    "both": ("sbuf", [128, 2 * COLS], "bfloat16"),
    "off": ("sbuf", [128, K], "uint16"),
    "res": ("sbuf", [128, M], "bfloat16"),
    "own": ("sbuf", [128, K], "uint16"),
    "land": ("sbuf", [128, 3 * M], "bfloat16"),
    "ia": ("sbuf", [128, K], "int32"),
    "pb": ("sbuf", [128, K], "int32"),
    "ib": ("sbuf", [128, K], "int32"),
    "o2": ("sbuf", [128, K], "int32"),
    "off2": ("sbuf", [128, K], "uint16"),
    "yb": ("sbuf", [128, M], "bfloat16"),
}
SEMAPHORES = ["s_idx", "s_ix", "s_io", "s_ej", "s_j1", "s_j2", "s_own", "s_o1", "s_o2", "s_o3", "s_o4", "s_og",
              "s_fw", "s_rq", "s_t0", "s_tab", "s_cv", "s_res", "s_land", "s_y", "s_st", "s_loc"] \
             + ["s_x%d" % i for i in range(CH)]


def _plan(T, topo):
    ranks = list(T.cores)
    chips = sorted(set(topo.chip(c) for c in ranks))
    assert len(chips) == 2
    on = {ch: [c for c in ranks if topo.chip(c) == ch] for ch in chips}
    near, far, helper = {}, {}, {}
    for s in ranks:
        near[s] = on[topo.chip(s)]
        far[s] = on[[ch for ch in chips if ch != topo.chip(s)][0]]
        assert len(near[s]) == 2 and T.rank_of(near[s][1]) == T.rank_of(near[s][0]) + 1
        cand = [h for h in range(topo.CORES_PER_CHIP * topo.CHIPS)
                if topo.chip(h) == topo.chip(s) and topo.die(h) == topo.die(s) and h not in ranks
                and h not in helper.values() and all(topo.may_write(h, t) for t in far[s])]
        helper[s] = cand[0]
    return near, far, helper


def _mask(topo, src, dst, lo, n):
    m = topo.mask(src, dst)
    es = [e for e in range(m.bit_length()) if (m >> e) & 1]
    assert lo + n <= len(es)
    return sum(1 << e for e in es[lo:lo + n])


def _width(topo, src, dst):
    m = topo.mask(src, dst)
    return sum((m >> e) & 1 for e in range(m.bit_length()))


def _xfer(topo, src, dst, lo, n, sem, out_ap, in_ap):
    rid, pid, _se = topo.addr(dst)
    return RemoteDMATransfer(dst_ids=[DstId(rid=rid, pnc=pid)], dma_engine_mask=_mask(topo, src, dst, lo, n),
                             remote_sem=sem, src=in_ap, dst=out_ap)


def _send(g, topo, src, dst, n, sem, loc, out_ap, in_ap):
    rid, pid, _se = topo.addr(dst)
    g.remote_dma(out_ap, in_ap, sem, loc, pid, rid, _mask(topo, src, dst, 0, n))
    return n


def _gather2(g, out, win, offs, waits, sem):
    for q in (g.vector, g.scalar):
        for s, n in waits:
            q.wait_ge(s, n)
    g.vector.tensor_copy(out[:, 0:M // 2], win.indirect(offs[:, 0:K // 2])).then_inc(sem, 1)
    g.scalar.activation(out[:, M // 2:M], win.indirect(offs[:, K // 2:K]), ActivationFunctionType.Copy,
                        bias=-0.0, scale=1.0).then_inc(sem, 1)


def _answer(g, T, win, first, span, n_rq, tab_waits):
    S, V = T.sem, g.vector
    V.wait_ge(S.s_rq, n_rq)
    V.tensor_scalar(T.off[:], T.rq[:], first, span - 1, AluOpType.subtract, AluOpType.min).then_inc(S.s_cv, 1)
    _gather2(g, T.res, win, T.off, tab_waits + [(S.s_cv, 1)], S.s_res)


def _slot(T, near, asker, owner):
    n0, o = T.rank_of(near[asker][0]), T.rank_of(owner)
    if owner in near[asker]:
        return o - n0 + (1 if n0 > 0 else 0)
    return 0 if n0 > 0 else 2


def _helper(g, core, T, topo, near, s, t, partner, other):
    S = T.sem
    w = _width(topo, core, partner)
    peer = [c for c in near[s] if c != s][0]
    a = M * _slot(T, near, t, s)
    b = near[s].index(s) * COLS
    g.iota(T.ia[:], [[16, K]], 0, 1).then_inc(S.s_io, 1)
    g.wait_ge(S.s_io, 1)
    loc = _send(g, topo, core, s, _width(topo, core, s), S.s_ej, S.s_loc, T.ia[:], T.ia[:])
    g.wait_ge(S.s_fw, E1)
    loc += _send(g, topo, core, partner, w, S.s_rq, S.s_loc, T.rq[:], T.ixd[:])
    loc += _send(g, topo, core, peer, EN, S.s_rq, S.s_loc, T.rq[:], T.ixd[:])
    wo = _width(topo, core, other)
    g.wait_ge(S.s_t0, _width(topo, s, core))
    loc += _send(g, topo, core, other, wo, S.s_tab, S.s_loc, T.both[:, b:b + PIECE], T.both[:, b:b + PIECE])
    _answer(g, T, T.both[:, 0:2 * COLS], COLS * T.rank_of(near[s][0]), 2 * COLS, w,
            [(S.s_t0, _width(topo, s, core)), (S.s_tab, _width(topo, other, core) + 2 * EX)])
    g.wait_ge(S.s_res, 2)
    loc += _send(g, topo, core, t, w, S.s_land, S.s_loc, T.land[:, a:a + M], T.res[:])
    g.wait_ge(S.s_loc, loc)


def _rank(g, core, T, topo, near, far, helper):
    S, V = T.sem, g.vector
    r = T.rank_of(core)
    place = near[core].index(core)
    hs = [helper[core]] + [helper[c] for c in near[core] if c != core]
    peer = [c for c in near[core] if c != core][0]
    sx = [S["s_x%d" % i] for i in range(CH)]
    wp = _width(topo, core, peer)

    g.sync.dma_start(T.ixd[:], T.idx[:]).then_inc(S.s_idx, 16)
    for i in range(CH):
        q = g.sync if i % 2 else g.scalar
        q.dma_start(T.tab[:, i * PIECE:(i + 1) * PIECE], T.x[:, i * PIECE:(i + 1) * PIECE]).then_inc(sx[i], 16)
    g.scalar.dma_start(T.ix[:], T.idx[:]).then_inc(S.s_ix, 16)

    g.iota(T.pb[:], [[0, K]], 0, 1).then_inc(S.s_io, 1)
    g.wait_ge(S.s_io, 1)
    loc = _send(g, topo, core, peer, wp, S.s_ej, S.s_loc, T.ib[:], T.pb[:])

    g.wait_ge(S.s_idx, 16)
    loc += _send(g, topo, core, hs[0], E1, S.s_fw, S.s_loc, T.ixd[:], T.ixd[:])
    b = place * COLS
    g.wait_ge(sx[0], 16)
    loc += _send(g, topo, core, hs[0], _width(topo, core, hs[0]), S.s_t0, S.s_loc,
                 T.both[:, b:b + PIECE], T.tab[:, 0:PIECE])
    g.wait_ge(sx[1], 16)
    g.remote_dma_fused([_xfer(topo, core, h, EX * i, EX, S.s_tab, T.both[:, b + PIECE:b + COLS], T.tab[:, PIECE:COLS])
                        for i, h in enumerate(hs)], local_sem=S.s_loc)
    loc += EX * len(hs)

    V.wait_ge(S.s_ej, _width(topo, hs[0], core) + _width(topo, peer, core))
    V.tensor_scalar(T.ib[:], T.ib[:], 0x70, None, AluOpType.bitwise_and).then_inc(S.s_j1, 1)
    V.wait_ge(S.s_j1, 1)
    V.tensor_tensor(T.ia[:], T.ia[:], T.ib[:], AluOpType.subtract).then_inc(S.s_j2, 1)
    V.wait_ge(S.s_ix, 16)
    V.tensor_scalar(T.own[:], T.ix[:], COLS * r, COLS - 1, AluOpType.subtract, AluOpType.min).then_inc(S.s_own, 1)
    V.tensor_scalar(T.o2[:], T.ix[:], 3, 0x700, AluOpType.arith_shift_right, AluOpType.bitwise_and).then_inc(S.s_o1, 1)
    V.wait_ge(S.s_o1, 1)
    if T.rank_of(near[core][0]) > 0:
        V.tensor_scalar(T.o2[:], T.o2[:], M, M, AluOpType.max, AluOpType.subtract).then_inc(S.s_o2, 1)
    else:
        V.tensor_scalar(T.o2[:], T.o2[:], 2 * M, None, AluOpType.min).then_inc(S.s_o2, 1)
    V.wait_ge(S.s_o2, 1)
    V.wait_ge(S.s_j2, 1)
    V.tensor_tensor(T.o2[:], T.o2[:], T.ia[:], AluOpType.add).then_inc(S.s_o3, 1)
    V.wait_ge(S.s_o3, 1)
    V.tensor_copy(T.off2[:], T.o2[:]).then_inc(S.s_o4, 1)
    a = M * _slot(T, near, core, core)
    V.wait_ge(S.s_own, 1)
    for sem in sx:
        V.wait_ge(sem, 16)
    V.tensor_copy(T.land[:, a:a + M], T.tab[:, 0:COLS].indirect(T.own[:, 0:K])).then_inc(S.s_og, 1)
    _answer(g, T, T.tab[:, 0:COLS], COLS * r, COLS, EN, [(sem, 16) for sem in sx])
    g.wait_ge(S.s_res, 2)
    a = M * _slot(T, near, peer, core)
    loc += _send(g, topo, core, peer, wp, S.s_land, S.s_loc, T.land[:, a:a + M], T.res[:])

    arrivals = _width(topo, peer, core) + _width(topo, helper[far[core][place]], core)
    _gather2(g, T.yb, T.land[:, 0:3 * M], T.off2, [(S.s_og, 1), (S.s_o4, 1), (S.s_land, arrivals)], S.s_y)
    g.sync.wait_ge(S.s_y, 2)
    g.sync.dma_start(T.y[:], T.yb[:]).then_inc(S.s_st, 16)
    g.sync.wait_ge(S.s_st, 16)
    g.wait_ge(S.s_loc, loc)


def rank_program(g, core, T, topo):
    near, far, helper = _plan(T, topo)
    if T.rank_of(core) is not None:
        _rank(g, core, T, topo, near, far, helper)
        return
    for s in T.cores:
        if helper[s] == core:
            t = far[s][near[s].index(s)]
            peer = [c for c in near[s] if c != s][0]
            _helper(g, core, T, topo, near, s, t, helper[t], helper[peer])
